import numpy as np
import ml_dtypes


def mxq(x, axis, fmt="e4m3"):
    dtype, down = {"e4m3": (ml_dtypes.float8_e4m3fn, 7), "e5m2": (ml_dtypes.float8_e5m2, 14)}[fmt]
    v = np.moveaxis(np.asarray(x, np.float32).astype(ml_dtypes.bfloat16).astype(np.float64), axis, -1)
    blocks = v.reshape(v.shape[:-1] + (-1, 32))
    amax = np.abs(blocks).max(-1, keepdims=True)
    byte = np.maximum(np.where(amax > 0, np.frexp(amax)[1] - 1 + 127, 0) - down, 1)
    scale = np.exp2(byte - 127.0)
    codes = (blocks / scale).astype(np.float32).astype(dtype).astype(np.float64)
    return np.moveaxis((codes * scale).reshape(v.shape), -1, axis)


WIDE = False


def mx_kscale(k):
    if not WIDE:
        return np.ones(k)
    levels = np.array([10, -10, 5, -5, 0])
    if k % 512:
        return np.exp2(np.random.permutation(np.resize(levels, k // 32))).repeat(32)
    a = np.empty((k // 512, 16))
    for p in range(k // 512):
        a[p, :8] = np.random.permutation(np.resize(levels, 8))
        for g in range(8):
            far = levels[np.abs(levels - a[p, g]) >= 10]
            a[p, g + 8] = far[np.random.randint(len(far))]
    return np.exp2(a.ravel()).repeat(32)


BF16 = ml_dtypes.bfloat16


def bf(x):
    return np.asarray(x, np.float32).astype(BF16)


def f64(x):
    return np.asarray(x).astype(np.float64)

E4M3FN = np.array([(-1.0 if i & 128 else 1.0) * ((1.0 + (i & 7) / 8.0) * 2.0 ** (((i >> 3) & 15) - 7) if i & 120 else (i & 7) * 2.0 ** -9) for i in range(256)])


def e4m3fn_bytes(y):
    return np.clip(np.asarray(y, np.float64), -448.0, 448.0).astype(np.float32).astype(ml_dtypes.float8_e4m3fn).view(np.uint8)


def e4m3fn_values(b):
    return E4M3FN[b]


T, K, N, G = 1024, 2048, 1536, 128


def setup_inputs():
    s = mx_kscale(K)
    field = 8.0 * np.random.standard_normal((T, K)) * s
    extent = np.random.uniform(0.5, 2.0, (N, 1))
    shared = extent * np.random.standard_exponential((N, K)) / K
    overlap = shared / s
    field_scale = (np.abs(field).reshape(T, K // G, G).max(axis=2) / 448.0).astype(np.float32)
    overlap_scale = (np.abs(overlap).reshape(N // G, G, K // G, G).max(axis=(1, 3)) / 448.0).astype(np.float32)
    return {"field_bytes": e4m3fn_bytes(field / np.repeat(f64(field_scale), G, axis=1)),
            "field_scale": field_scale,
            "overlap_bytes": e4m3fn_bytes(overlap / np.repeat(np.repeat(f64(overlap_scale), G, axis=0), G, axis=1)),
            "overlap_scale": overlap_scale,
            "area": bf(shared.sum(axis=1)),
            "clim": bf(0.3 * np.random.standard_normal(N))}


def reference(field_bytes, field_scale, overlap_bytes, overlap_scale, area, clim):
    field = e4m3fn_values(field_bytes) * np.repeat(f64(field_scale), G, axis=1)
    overlap = e4m3fn_values(overlap_bytes) * np.repeat(np.repeat(f64(overlap_scale), G, axis=0), G, axis=1)
    total = mxq(field, 1, "e4m3") @ mxq(overlap, 1, "e4m3").T
    return total / f64(area) + f64(clim)

@@ -1,0 +1,221 @@
+from contextlib import ExitStack
+
+import concourse.mybir as mybir
+from concourse.masks import make_identity
+
+T, K, N = 1024, 2048, 1536
+P = 128
+FLOPS = 2 * T * K * N
+
+F32 = mybir.dt.float32
+BF16 = mybir.dt.bfloat16
+U8 = mybir.dt.uint8
+U32 = mybir.dt.uint32
+FP8 = mybir.dt.float8_e4m3fn
+FP8X4 = mybir.dt.float8_e4m3fn_x4
+COPY = mybir.ActivationFunctionType.Copy
+MULT = mybir.AluOpType.mult
+ADD = mybir.AluOpType.add
+
+UNITS = ["W0", "F0", "F1", "W1", "F2", "F3", "W2", "W3", "F4", "F5", "W4", "W5", "F6", "F7"]
+TR_LAG, EXIT_LAG, QUANT_LAG = 2, 4, 5
+
+
+def tile_area_overlap_regridding_d2_kernel(
+    tc, field_bytes, field_scale, overlap_bytes, overlap_scale, area, clim, out
+):
+    nc = tc.nc
+    with ExitStack() as ctx:
+        keep = ctx.enter_context(tc.tile_pool(name="keep", bufs=1))
+        wide_pool = ctx.enter_context(tc.tile_pool(name="wide", bufs=6))
+        group_pool = ctx.enter_context(tc.tile_pool(name="grouped", bufs=4))
+        res_pool = ctx.enter_context(tc.tile_pool(name="res", bufs=6))
+        psum_tr = ctx.enter_context(tc.psum_pool(name="psum_tr", bufs=4))
+        psum_acc = ctx.enter_context(tc.psum_pool(name="psum_acc", bufs=4))
+
+        ident = keep.tile([P, P], F32, name="ident")
+        make_identity(nc, ident[:])
+        area_f32 = keep.tile([P, P], F32, name="area_f32")
+        nc.gpsimd.memset(area_f32[:], 0.0)
+
+        f_scale = keep.tile([P, 8, 16], F32, name="f_scale")
+        o_scale = keep.tile([P, 192], F32, name="o_scale")
+        area_rows = keep.tile([12, P], BF16, name="area_rows")
+        clim_all = keep.tile([P, N], BF16, name="clim_all")
+        inv_cols = keep.tile([P, 12], F32, name="inv_cols")
+        inv_all = keep.tile([P, N], F32, name="inv_all")
+
+        nc.scalar.dma_start(out=o_scale[:], in_=overlap_scale.rearrange("a b -> (a b)").partition_broadcast(P))
+        nc.scalar.dma_start(out=f_scale[:], in_=field_scale.rearrange("(m p) b -> p m b", p=P))
+        nc.scalar.dma_start(out=area_rows[:], in_=area.rearrange("(c p) -> c p", p=P))
+
+        raw = {}
+        for n, u in enumerate(UNITS):
+            i = int(u[1:])
+            if u[0] == "W":
+                t = keep.tile([P, 2, K], U8, name="w_bytes%d" % i)
+                src = overlap_bytes[256 * i : 256 * i + 256, :].rearrange("(t p) k -> p t k", p=P)
+                if n == 0:
+                    nc.sync.dma_start(out=t[:, :, 0:512], in_=src[:, :, 0:512])
+                    nc.sync.dma_start(out=t[:, :, 512:K], in_=src[:, :, 512:K])
+                else:
+                    nc.sync.dma_start(out=t[:], in_=src)
+            else:
+                t = keep.tile([P, K], U8, name="f_bytes%d" % i)
+                nc.sync.dma_start(out=t[:], in_=field_bytes[P * i : P * i + P, :])
+            raw[u] = t
+            if n == 5:
+                nc.sync.dma_start(out=clim_all[:], in_=clim.partition_broadcast(P))
+
+        w_codes = [keep.tile([P, 4, 512], U32, align_bytes=64, name="w_codes%d" % j) for j in range(3)]
+        w_planes = [keep.tile([P, 4, 512], U8, align_bytes=64, name="w_planes%d" % j) for j in range(3)]
+        f_codes = [keep.tile([P, 4, P], U32, align_bytes=64, name="f_codes%d" % m) for m in range(8)]
+        f_planes = [keep.tile([P, 4, P], U8, align_bytes=64, name="f_planes%d" % m) for m in range(8)]
+
+        chunks = []
+        for u in UNITS:
+            chunks += [(u, c) for c in range(4 if u[0] == "W" else 2)]
+        n_chunks = len(chunks)
+        wide, bank, grouped = {}, {}, {}
+
+        def widen(c):
+            u, part = chunks[c]
+            i = int(u[1:])
+            for h in (0, 1):
+                on_scalar = h == 0 or (c >= 36 and c % 2 == 0)
+                t = wide_pool.tile([P, 512], BF16, align_bytes=64, name="wide%d" % h)
+                for q in range(4):
+                    if u[0] == "W":
+                        b = 4 * part + q
+                        src = raw[u][:, h, P * b : P * b + P]
+                        col = o_scale[:, 16 * (2 * i + h) + b : 16 * (2 * i + h) + b + 1]
+                    else:
+                        b = 4 * (2 * part + h) + q
+                        src = raw[u][:, P * b : P * b + P]
+                        col = f_scale[:, i, b : b + 1]
+                    dst = t[:, P * q : P * q + P]
+                    if on_scalar:
+                        nc.scalar.activation(out=dst, in_=src.bitcast(FP8), func=COPY, scale=col)
+                    else:
+                        nc.vector.tensor_scalar(out=dst, in0=src.bitcast(FP8), scalar1=col, scalar2=None, op0=MULT)
+                wide[c, h] = t
+
+        def turn(c):
+            t = psum_tr.tile([P, 2, 2, P], F32, name="bank")
+            for h in (0, 1):
+                words = wide[c, h][:].bitcast(F32)
+                for e in (0, 1):
+                    nc.tensor.transpose(t[:, h, e, :], words[:, e::2], ident[:])
+            bank[c] = t
+
+        def leave(c):
+            t = group_pool.tile([P, 2, P, 4], BF16, align_bytes=64, name="group")
+            dst = t[:].rearrange("p h r t -> p (h r t)").bitcast(F32).rearrange("p (h r e) -> p h r e", h=2, e=2)
+            src = bank[c][:].rearrange("p h e r -> p h r e")
+            if c < 16 and c % 3 == 2:
+                nc.vector.tensor_copy(out=dst, in_=src)
+            else:
+                nc.scalar.copy(out=dst, in_=src)
+            grouped[c] = t
+
+        def quantize(c):
+            u, part = chunks[c]
+            i = int(u[1:])
+            if u[0] == "W":
+                cols = slice(256 * (i % 2), 256 * (i % 2) + 256)
+                codes = w_codes[i // 2][:, part, cols]
+                planes = w_planes[i // 2][:, part, cols]
+            else:
+                codes = f_codes[i][:, 2 * part : 2 * part + 2, :].rearrange("p g r -> p (g r)")
+                planes = f_planes[i][:, 2 * part : 2 * part + 2, :].rearrange("p g r -> p (g r)")
+            nc.vector.quantize_mx(
+                out=codes.bitcast(FP8X4), scales=planes, in_=grouped[c][:].rearrange("p h r t -> p (h r t)")
+            )
+
+        def multiply(m, j, lo, width):
+            acc = psum_acc.tile([P, 512], F32, name="acc")
+            for g in range(4):
+                nc.tensor.matmul_mx(
+                    out=acc[:, 0:width],
+                    lhsT=f_codes[m][:, g, :].bitcast(FP8X4),
+                    lhsT_scale=f_planes[m][:, g, :],
+                    rhs=w_codes[j][:, g, lo : lo + width].bitcast(FP8X4),
+                    rhs_scale=w_planes[j][:, g, lo : lo + width],
+                    start=(g == 0),
+                    stop=(g == 3),
+                )
+            return acc
+
+        def area_columns():
+            nc.vector.tensor_copy(out=area_f32[0:12, :], in_=area_rows[:])
+            t = psum_tr.tile([P, 4, P], F32, name="bank")
+            nc.tensor.transpose(t[:, 0, :], area_f32[:], ident[:])
+            nc.vector.reciprocal(out=inv_cols[:], in_=t[:, 0, 0:12])
+
+        def spread_inverse():
+            for j in range(3):
+                t = psum_tr.tile([P, 4, P], F32, name="bank")
+                for c in range(4):
+                    col = 4 * j + c
+                    nc.tensor.transpose(t[:, c, :], inv_cols[:, col : col + 1].to_broadcast([P, P]), ident[:])
+                nc.scalar.copy(out=inv_all[:, 512 * j : 512 * j + 512], in_=t[:].rearrange("p c r -> p (c r)"))
+
+        with tc.manual_schedule():
+            ready, to_scale, to_add = [], [], []
+            done_f, done_w = [], []
+            credit = 0.0
+            step = 0
+            while step < n_chunks + QUANT_LAG or ready or to_scale or to_add:
+                if step == 4:
+                    area_columns()
+                if step == 7:
+                    spread_inverse()
+                if 0 <= step - EXIT_LAG < n_chunks:
+                    leave(step - EXIT_LAG)
+                if step < n_chunks:
+                    widen(step)
+                fresh = []
+                c = step - QUANT_LAG
+                if 0 <= c < n_chunks:
+                    quantize(c)
+                    u = chunks[c][0]
+                    if c + 1 == n_chunks or chunks[c + 1][0] != u:
+                        i = int(u[1:])
+                        if u[0] == "W":
+                            fresh = [(m, i // 2, 256 * (i % 2), 256) for m in done_f]
+                            done_w.append(i)
+                        else:
+                            for j in range(3):
+                                if 2 * j in done_w and 2 * j + 1 in done_w:
+                                    fresh.append((i, j, 0, 512))
+                                elif 2 * j in done_w:
+                                    fresh.append((i, j, 0, 256))
+                            done_f.append(i)
+                for m, j, lo, width, res in to_add:
+                    nc.vector.tensor_tensor(
+                        out=res[:, 0:width], in0=res[:, 0:width],
+                        in1=clim_all[:, 512 * j + lo : 512 * j + lo + width], op=ADD,
+                    )
+                    nc.sync.dma_start(
+                        out=out[P * m : P * m + P, 512 * j + lo : 512 * j + lo + width], in_=res[:, 0:width]
+                    )
+                to_add = []
+                for m, j, lo, width, acc in to_scale:
+                    res = res_pool.tile([P, 512], F32, name="res")
+                    nc.vector.tensor_tensor(
+                        out=res[:, 0:width], in0=acc[:, 0:width],
+                        in1=inv_all[:, 512 * j + lo : 512 * j + lo + width], op=MULT,
+                    )
+                    to_add.append((m, j, lo, width, res))
+                to_scale = []
+                c = step - TR_LAG
+                if 0 <= c < n_chunks and c % 2 == 1:
+                    turn(c - 1)
+                    turn(c)
+                credit = min(credit + 1.5, 6.0) if ready else 1.0
+                while ready and credit >= ready[0][3] / 256:
+                    m, j, lo, width = ready.pop(0)
+                    credit -= width / 256
+                    to_scale.append((m, j, lo, width, multiply(m, j, lo, width)))
+                ready += fresh
+                step += 1

@@ -17,8 +17,8 @@ COPY = mybir.ActivationFunctionType.Copy
 MULT = mybir.AluOpType.mult
 ADD = mybir.AluOpType.add
 
-UNITS = ["W0", "F0", "F1", "W1", "F2", "F3", "W2", "W3", "F4", "F5", "W4", "W5", "F6", "F7"]
-TR_LAG, EXIT_LAG, QUANT_LAG = 2, 4, 5
+CFG = {"units":["W0","F0","F1","W1","F2","F3","W2","W3","F4","F5","W4","W5","F6","F7"],"v":[6,4,4],"b":[20,28],"contig":0,"nt":4,"g":[],"x":[2,5],"TL":2,"EL":4,"QL":5,"R":2,"inv":6,"sfirst":1,"vorder":"qwo","tfirst":1,"pace":[0.6,2],"ps":40}
+UNITS = CFG["units"]
 
 
 def tile_area_overlap_regridding_d2_kernel(
@@ -27,11 +27,11 @@ def tile_area_overlap_regridding_d2_kernel(
     nc = tc.nc
     with ExitStack() as ctx:
         keep = ctx.enter_context(tc.tile_pool(name="keep", bufs=1))
-        wide_pool = ctx.enter_context(tc.tile_pool(name="wide", bufs=6))
-        group_pool = ctx.enter_context(tc.tile_pool(name="grouped", bufs=4))
-        res_pool = ctx.enter_context(tc.tile_pool(name="res", bufs=6))
-        psum_tr = ctx.enter_context(tc.psum_pool(name="psum_tr", bufs=4))
-        psum_acc = ctx.enter_context(tc.psum_pool(name="psum_acc", bufs=4))
+        wide_pool = ctx.enter_context(tc.tile_pool(name="wide", bufs=24))
+        group_pool = ctx.enter_context(tc.tile_pool(name="grouped", bufs=6))
+        res_pool = ctx.enter_context(tc.tile_pool(name="res", bufs=8))
+        psum_tr = ctx.enter_context(tc.psum_pool(name="psum_tr", bufs=CFG["nt"]))
+        psum_acc = ctx.enter_context(tc.psum_pool(name="psum_acc", bufs=8 - CFG["nt"]))
 
         ident = keep.tile([P, P], F32, name="ident")
         make_identity(nc, ident[:])
@@ -46,107 +46,158 @@ def tile_area_overlap_regridding_d2_kernel(
         inv_all = keep.tile([P, N], F32, name="inv_all")
 
         nc.scalar.dma_start(out=o_scale[:], in_=overlap_scale.rearrange("a b -> (a b)").partition_broadcast(P))
-        nc.scalar.dma_start(out=f_scale[:], in_=field_scale.rearrange("(m p) b -> p m b", p=P))
+        nc.scalar.dma_start(out=f_scale[:], in_=field_scale.rearrange("(p m) b -> p m b", m=8))
         nc.scalar.dma_start(out=area_rows[:], in_=area.rearrange("(c p) -> c p", p=P))
 
-        raw = {}
-        for n, u in enumerate(UNITS):
-            i = int(u[1:])
-            if u[0] == "W":
-                t = keep.tile([P, 2, K], U8, name="w_bytes%d" % i)
-                src = overlap_bytes[256 * i : 256 * i + 256, :].rearrange("(t p) k -> p t k", p=P)
-                if n == 0:
-                    nc.sync.dma_start(out=t[:, :, 0:512], in_=src[:, :, 0:512])
-                    nc.sync.dma_start(out=t[:, :, 512:K], in_=src[:, :, 512:K])
-                else:
-                    nc.sync.dma_start(out=t[:], in_=src)
-            else:
-                t = keep.tile([P, K], U8, name="f_bytes%d" % i)
-                nc.sync.dma_start(out=t[:], in_=field_bytes[P * i : P * i + P, :])
-            raw[u] = t
-            if n == 5:
-                nc.sync.dma_start(out=clim_all[:], in_=clim.partition_broadcast(P))
+        w_bytes = [keep.tile([P, 2, K], U8, name="w_bytes%d" % i) for i in range(6)]
+        f_bytes = [keep.tile([P, 2, K], U8, name="f_bytes%d" % i) for i in range(4)]
+        f_rows = field_bytes.rearrange("(p m) k -> p m k", m=8)
 
-        w_codes = [keep.tile([P, 4, 512], U32, align_bytes=64, name="w_codes%d" % j) for j in range(3)]
-        w_planes = [keep.tile([P, 4, 512], U8, align_bytes=64, name="w_planes%d" % j) for j in range(3)]
+        def load_w(i, lo, hi):
+            src = overlap_bytes[256 * i : 256 * i + 256, lo:hi].rearrange("(t p) k -> p t k", p=P)
+            nc.sync.dma_start(out=w_bytes[i][:, :, lo:hi], in_=src)
+
+        def load_f(i):
+            nc.sync.dma_start(out=f_bytes[i][:], in_=f_rows[:, 2 * i : 2 * i + 2, :])
+
+        load_w(0, 0, 512)
+        load_w(0, 512, K)
+        load_f(0)
+        load_w(1, 0, K)
+        load_f(1)
+        load_w(2, 0, K)
+        load_w(3, 0, K)
+        nc.sync.dma_start(out=clim_all[:], in_=clim.partition_broadcast(P))
+        load_f(2)
+        load_w(4, 0, K)
+        load_w(5, 0, K)
+        load_f(3)
+
+        w_codes = [keep.tile([P, 4, 256], U32, align_bytes=64, name="w_codes%d" % i) for i in range(6)]
+        w_planes = [keep.tile([P, 4, 256], U8, align_bytes=64, name="w_planes%d" % i) for i in range(6)]
         f_codes = [keep.tile([P, 4, P], U32, align_bytes=64, name="f_codes%d" % m) for m in range(8)]
         f_planes = [keep.tile([P, 4, P], U8, align_bytes=64, name="f_planes%d" % m) for m in range(8)]
 
         chunks = []
         for u in UNITS:
-            chunks += [(u, c) for c in range(4 if u[0] == "W" else 2)]
+            chunks += [(u[0], int(u[1:]), c) for c in range(4 if u[0] == "W" else 2)]
         n_chunks = len(chunks)
         wide, bank, grouped = {}, {}, {}
 
-        def widen(c):
-            u, part = chunks[c]
-            i = int(u[1:])
-            for h in (0, 1):
-                on_scalar = h == 0 or (c >= 36 and c % 2 == 0)
-                t = wide_pool.tile([P, 512], BF16, align_bytes=64, name="wide%d" % h)
-                for q in range(4):
-                    if u[0] == "W":
-                        b = 4 * part + q
-                        src = raw[u][:, h, P * b : P * b + P]
-                        col = o_scale[:, 16 * (2 * i + h) + b : 16 * (2 * i + h) + b + 1]
-                    else:
-                        b = 4 * (2 * part + h) + q
-                        src = raw[u][:, P * b : P * b + P]
-                        col = f_scale[:, i, b : b + 1]
-                    dst = t[:, P * q : P * q + P]
-                    if on_scalar:
-                        nc.scalar.activation(out=dst, in_=src.bitcast(FP8), func=COPY, scale=col)
-                    else:
-                        nc.vector.tensor_scalar(out=dst, in0=src.bitcast(FP8), scalar1=col, scalar2=None, op0=MULT)
-                wide[c, h] = t
+        def on_vector(c, h):
+            share = CFG['v'][0] if c < CFG['b'][0] else CFG['v'][1] if c < CFG['b'][1] else CFG['v'][2]
+            j = 2 * c + 1 - h
+            return (j + 1) * share // 8 > j * share // 8
+
+        def widen(c, h):
+            kind, i, part = chunks[c]
+            t = wide_pool.tile([P, 512], BF16, align_bytes=64, name="wide")
+            for q in range(4):
+                if kind == "W":
+                    b = 4 * part + q
+                    src = w_bytes[i][:, h, P * b : P * b + P]
+                    col = o_scale[:, 16 * (2 * i + h) + b : 16 * (2 * i + h) + b + 1]
+                else:
+                    b = 4 * (2 * part + h) + q
+                    src = f_bytes[i // 2][:, i % 2, P * b : P * b + P]
+                    col = f_scale[:, i, b : b + 1]
+                dst = t[:, P * q : P * q + P]
+                if on_vector(c, h):
+                    nc.vector.tensor_scalar(
+                        out=t[:].rearrange("p (e w i) -> p w e i", e=2, i=2)[:, 32 * q : 32 * q + 32] if CFG["contig"] else dst,
+                        in0=src.bitcast(FP8).rearrange("p (w e i) -> p w e i", e=2, i=2) if CFG["contig"] else src.bitcast(FP8),
+                        scalar1=col, scalar2=None, op0=MULT,
+                    )
+                else:
+                    nc.scalar.activation(out=dst, in_=src.bitcast(FP8), func=COPY, scale=col)
+            wide[c, h] = t
 
         def turn(c):
             t = psum_tr.tile([P, 2, 2, P], F32, name="bank")
             for h in (0, 1):
                 words = wide[c, h][:].bitcast(F32)
+                split = CFG['contig'] and on_vector(c, h)
                 for e in (0, 1):
-                    nc.tensor.transpose(t[:, h, e, :], words[:, e::2], ident[:])
+                    nc.tensor.transpose(t[:, h, e, :], words[:, P * e : P * e + P] if split else words[:, e::2], ident[:])
             bank[c] = t
 
         def leave(c):
-            t = group_pool.tile([P, 2, P, 4], BF16, align_bytes=64, name="group")
-            dst = t[:].rearrange("p h r t -> p (h r t)").bitcast(F32).rearrange("p (h r e) -> p h r e", h=2, e=2)
-            src = bank[c][:].rearrange("p h e r -> p h r e")
-            if c < 16 and c % 3 == 2:
-                nc.vector.tensor_copy(out=dst, in_=src)
+            if c % 2 == 0:
+                grouped[c] = group_pool.tile([P, 2, 1024], BF16, align_bytes=64, name="group")
+            t = grouped[c - c % 2]
+            dst = t[:, c % 2, :].bitcast(F32).rearrange("p (h r e) -> p h r e", h=2, e=2)
+            if c in CFG['x']:
+                nc.vector.tensor_copy(out=dst, in_=bank[c][:].rearrange("p h e r -> p h r e"))
             else:
-                nc.scalar.copy(out=dst, in_=src)
-            grouped[c] = t
+                nc.scalar.copy(out=dst, in_=bank[c][:].rearrange("p h e r -> p h r e"))
 
-        def quantize(c):
-            u, part = chunks[c]
-            i = int(u[1:])
-            if u[0] == "W":
-                cols = slice(256 * (i % 2), 256 * (i % 2) + 256)
-                codes = w_codes[i // 2][:, part, cols]
-                planes = w_planes[i // 2][:, part, cols]
-            else:
-                codes = f_codes[i][:, 2 * part : 2 * part + 2, :].rearrange("p g r -> p (g r)")
-                planes = f_planes[i][:, 2 * part : 2 * part + 2, :].rearrange("p g r -> p (g r)")
-            nc.vector.quantize_mx(
-                out=codes.bitcast(FP8X4), scales=planes, in_=grouped[c][:].rearrange("p h r t -> p (h r t)")
-            )
-
-        def multiply(m, j, lo, width):
-            acc = psum_acc.tile([P, 512], F32, name="acc")
-            for g in range(4):
-                nc.tensor.matmul_mx(
-                    out=acc[:, 0:width],
-                    lhsT=f_codes[m][:, g, :].bitcast(FP8X4),
-                    lhsT_scale=f_planes[m][:, g, :],
-                    rhs=w_codes[j][:, g, lo : lo + width].bitcast(FP8X4),
-                    rhs_scale=w_planes[j][:, g, lo : lo + width],
-                    start=(g == 0),
-                    stop=(g == 3),
-                )
+        def multiply(ms, qs):
+            acc = psum_acc.tile([P, 2, 256], F32, name="acc")
+            for half, (m, q) in enumerate([(m, q) for m in ms for q in qs]):
+                for g in range(4):
+                    nc.tensor.matmul_mx(
+                        out=acc[:, half, :],
+                        lhsT=f_codes[m][:, g, :].bitcast(FP8X4),
+                        lhsT_scale=f_planes[m][:, g, :],
+                        rhs=w_codes[q][:, g, :].bitcast(FP8X4),
+                        rhs_scale=w_planes[q][:, g, :],
+                        start=(g == 0),
+                        stop=(g == 3),
+                    )
             return acc
 
-        def area_columns():
+        ready, done_f, done_w = [], [], []
+
+        def quantize(c):
+            kind, i, part = chunks[c]
+            if kind == "W":
+                codes = w_codes[i][:, part : part + 2, :].rearrange("p g r -> p (g r)")
+                planes = w_planes[i][:, part : part + 2, :].rearrange("p g r -> p (g r)")
+            else:
+                codes = f_codes[i][:].rearrange("p g r -> p (g r)")
+                planes = f_planes[i][:].rearrange("p g r -> p (g r)")
+            nc.vector.quantize_mx(
+                out=codes.bitcast(FP8X4), scales=planes, in_=grouped[c][:].rearrange("p c x -> p (c x)")
+            )
+            if kind == "W" and part == 2:
+                done_w.append(i)
+                ready.extend([((m, m + 1), (i,)) for m in done_f if m % 2 == 0])
+            if kind == "F":
+                done_f.append(i)
+                if i >= 6:
+                    ready.extend([((i,), (2 * j, 2 * j + 1)) for j in range(3)])
+                elif i % 2 == 1:
+                    ready.extend([((i - 1, i), (q,)) for q in done_w])
+
+        def over_columns(row, qs, n_ms):
+            cols = row[:, 256 * qs[0] : 256 * qs[0] + 256 * len(qs)]
+            if n_ms == 2:
+                return cols.unsqueeze(1).to_broadcast([P, 2, 256])
+            return cols.rearrange("p (q n) -> p q n", q=2)
+
+        results, order = {}, {}
+
+        def scale(task, acc):
+            ms, qs = task
+            res = res_pool.tile([P, 2, 256], F32, name="res")
+            nc.vector.tensor_tensor(out=res[:], in0=acc[:], in1=over_columns(inv_all, qs, len(ms)), op=MULT)
+            results[task] = res
+            order[task] = len(order)
+
+        out_rows = out.rearrange("(p m) n -> p m n", m=8)
+
+        def shift(task):
+            ms, qs = task
+            res = results[task]
+            adder = nc.gpsimd if order[task] in CFG['g'] else nc.vector
+            adder.tensor_tensor(out=res[:], in0=res[:], in1=over_columns(clim_all, qs, len(ms)), op=ADD)
+            cols = slice(256 * qs[0], 256 * qs[0] + 256 * len(qs))
+            if len(ms) == 2:
+                nc.sync.dma_start(out=out_rows[:, ms[0] : ms[0] + 2, cols], in_=res[:])
+            else:
+                nc.sync.dma_start(out=out_rows[:, ms[0], cols], in_=res[:].rearrange("p q n -> p (q n)"))
+
+        def invert_area():
             nc.vector.tensor_copy(out=area_f32[0:12, :], in_=area_rows[:])
             t = psum_tr.tile([P, 4, P], F32, name="bank")
             nc.tensor.transpose(t[:, 0, :], area_f32[:], ident[:])
@@ -161,61 +212,48 @@ def tile_area_overlap_regridding_d2_kernel(
                 nc.scalar.copy(out=inv_all[:, 512 * j : 512 * j + 512], in_=t[:].rearrange("p c r -> p (c r)"))
 
         with tc.manual_schedule():
-            ready, to_scale, to_add = [], [], []
-            done_f, done_w = [], []
+            TL, EL, QL, R = CFG["TL"], CFG["EL"], CFG["QL"], CFG["R"]
+            fresh, last_shift, older = [], [], []
             credit = 0.0
             step = 0
-            while step < n_chunks + QUANT_LAG or ready or to_scale or to_add:
-                if step == 4:
-                    area_columns()
-                if step == 7:
+            while step < n_chunks + QL + 1 or ready or fresh or last_shift or older:
+                if step == CFG["inv"]:
+                    invert_area()
+                if step == CFG["inv"] + 3:
                     spread_inverse()
-                if 0 <= step - EXIT_LAG < n_chunks:
-                    leave(step - EXIT_LAG)
-                if step < n_chunks:
-                    widen(step)
+                groups = [(step, h) for h in (0, 1)] if step < n_chunks else []
+                sg = [g for g in groups if not on_vector(g[0], g[1])]
+                vg = [g for g in groups if on_vector(g[0], g[1])]
+                if CFG["sfirst"]:
+                    for g in sg[:1]:
+                        widen(g[0], g[1])
+                    sg = sg[1:]
+                if 0 <= step - EL < n_chunks:
+                    leave(step - EL)
+                for g in sg:
+                    widen(g[0], g[1])
+                able = len(ready)
+                c = step - QL
+                outs = [(shift, (t,)) for t in last_shift] + [(scale, z) for z in fresh]
+                last_shift = [z[0] for z in fresh]
+                quant = [(quantize, (c - 1,))] if 0 <= c < n_chunks and c % 2 == 1 else []
+                wid = [(widen, g) for g in vg]
+                for part in CFG["vorder"]:
+                    for fn, args in {"w": wid, "q": quant, "o": outs}[part]:
+                        fn(*args)
                 fresh = []
-                c = step - QUANT_LAG
-                if 0 <= c < n_chunks:
-                    quantize(c)
-                    u = chunks[c][0]
-                    if c + 1 == n_chunks or chunks[c + 1][0] != u:
-                        i = int(u[1:])
-                        if u[0] == "W":
-                            fresh = [(m, i // 2, 256 * (i % 2), 256) for m in done_f]
-                            done_w.append(i)
-                        else:
-                            for j in range(3):
-                                if 2 * j in done_w and 2 * j + 1 in done_w:
-                                    fresh.append((i, j, 0, 512))
-                                elif 2 * j in done_w:
-                                    fresh.append((i, j, 0, 256))
-                            done_f.append(i)
-                for m, j, lo, width, res in to_add:
-                    nc.vector.tensor_tensor(
-                        out=res[:, 0:width], in0=res[:, 0:width],
-                        in1=clim_all[:, 512 * j + lo : 512 * j + lo + width], op=ADD,
-                    )
-                    nc.sync.dma_start(
-                        out=out[P * m : P * m + P, 512 * j + lo : 512 * j + lo + width], in_=res[:, 0:width]
-                    )
-                to_add = []
-                for m, j, lo, width, acc in to_scale:
-                    res = res_pool.tile([P, 512], F32, name="res")
-                    nc.vector.tensor_tensor(
-                        out=res[:, 0:width], in0=acc[:, 0:width],
-                        in1=inv_all[:, 512 * j + lo : 512 * j + lo + width], op=MULT,
-                    )
-                    to_add.append((m, j, lo, width, res))
-                to_scale = []
-                c = step - TR_LAG
-                if 0 <= c < n_chunks and c % 2 == 1:
-                    turn(c - 1)
-                    turn(c)
-                credit = min(credit + 1.5, 6.0) if ready else 1.0
-                while ready and credit >= ready[0][3] / 256:
-                    m, j, lo, width = ready.pop(0)
-                    credit -= width / 256
-                    to_scale.append((m, j, lo, width, multiply(m, j, lo, width)))
-                ready += fresh
+                c = step - TL
+                turns = list(range(c - R + 1, c + 1)) if 0 <= c < n_chunks and c % R == R - 1 else []
+                if CFG["tfirst"]:
+                    for k in turns:
+                        turn(k)
+                credit = min(credit + (CFG["pace"][0] if step < CFG["ps"] else CFG["pace"][1]), 3.0) if ready else 0.5
+                while able > 0 and credit >= 1.0:
+                    task = ready.pop(0)
+                    able -= 1
+                    credit -= 1.0
+                    fresh.append((task, multiply(*task)))
+                if not CFG["tfirst"]:
+                    for k in turns:
+                        turn(k)
                 step += 1

@@ -17,7 +17,7 @@ COPY = mybir.ActivationFunctionType.Copy
 MULT = mybir.AluOpType.mult
 ADD = mybir.AluOpType.add
 
-CFG = {"units":["W0","F0","F1","W1","F2","F3","W2","W3","F4","F5","W4","W5","F6","F7"],"v":[6,4,4],"b":[20,28],"contig":0,"nt":4,"g":[],"x":[2,5],"TL":2,"EL":4,"QL":5,"R":2,"inv":6,"sfirst":1,"vorder":"qwo","tfirst":1,"pace":[0.6,2],"ps":40}
+CFG = {"units":["W0","F0","F1","F2","F3","W1","W2","F4","F5","W3","W4","W5","F6","F7"],"v":[5,4,3],"b":[20,28],"contig":1,"nt":5,"g":[],"x":[2,5],"TL":2,"EL":4,"QL":5,"R":2,"inv":6,"sfirst":0,"vorder":"wqo","tfirst":1,"pace":[0.6,2],"ps":40}
 UNITS = CFG["units"]
 
 
@@ -62,16 +62,13 @@ def tile_area_overlap_regridding_d2_kernel(
 
         load_w(0, 0, 512)
         load_w(0, 512, K)
-        load_f(0)
-        load_w(1, 0, K)
-        load_f(1)
-        load_w(2, 0, K)
-        load_w(3, 0, K)
-        nc.sync.dma_start(out=clim_all[:], in_=clim.partition_broadcast(P))
-        load_f(2)
-        load_w(4, 0, K)
-        load_w(5, 0, K)
-        load_f(3)
+        for u in UNITS[1:]:
+            if u == "W2":
+                nc.sync.dma_start(out=clim_all[:], in_=clim.partition_broadcast(P))
+            if u[0] == "W":
+                load_w(int(u[1:]), 0, K)
+            elif u[1:] in "0246":
+                load_f(int(u[1:]) // 2)
 
         w_codes = [keep.tile([P, 4, 256], U32, align_bytes=64, name="w_codes%d" % i) for i in range(6)]
         w_planes = [keep.tile([P, 4, 256], U8, align_bytes=64, name="w_planes%d" % i) for i in range(6)]

from contextlib import ExitStack

import concourse.mybir as mybir
from concourse.masks import make_identity

T, K, N = 1024, 2048, 1536
P = 128
FLOPS = 2 * T * K * N

F32 = mybir.dt.float32
BF16 = mybir.dt.bfloat16
U8 = mybir.dt.uint8
U32 = mybir.dt.uint32
FP8 = mybir.dt.float8_e4m3fn
FP8X4 = mybir.dt.float8_e4m3fn_x4
COPY = mybir.ActivationFunctionType.Copy
MULT = mybir.AluOpType.mult
ADD = mybir.AluOpType.add

CFG = {"units":["W0","F0","F1","F2","F3","W1","W2","F4","F5","W3","W4","W5","F6","F7"],"v":[5,4,3],"b":[20,28],"contig":1,"nt":5,"g":[],"x":[2,5],"TL":2,"EL":4,"QL":5,"R":2,"inv":6,"sfirst":0,"vorder":"wqo","tfirst":1,"pace":[0.6,2],"ps":40}
UNITS = CFG["units"]


def tile_area_overlap_regridding_d2_kernel(
    tc, field_bytes, field_scale, overlap_bytes, overlap_scale, area, clim, out
):
    nc = tc.nc
    with ExitStack() as ctx:
        keep = ctx.enter_context(tc.tile_pool(name="keep", bufs=1))
        wide_pool = ctx.enter_context(tc.tile_pool(name="wide", bufs=24))
        group_pool = ctx.enter_context(tc.tile_pool(name="grouped", bufs=6))
        res_pool = ctx.enter_context(tc.tile_pool(name="res", bufs=8))
        psum_tr = ctx.enter_context(tc.psum_pool(name="psum_tr", bufs=CFG["nt"]))
        psum_acc = ctx.enter_context(tc.psum_pool(name="psum_acc", bufs=8 - CFG["nt"]))

        ident = keep.tile([P, P], F32, name="ident")
        make_identity(nc, ident[:])
        area_f32 = keep.tile([P, P], F32, name="area_f32")
        nc.gpsimd.memset(area_f32[:], 0.0)

        f_scale = keep.tile([P, 8, 16], F32, name="f_scale")
        o_scale = keep.tile([P, 192], F32, name="o_scale")
        area_rows = keep.tile([12, P], BF16, name="area_rows")
        clim_all = keep.tile([P, N], BF16, name="clim_all")
        inv_cols = keep.tile([P, 12], F32, name="inv_cols")
        inv_all = keep.tile([P, N], F32, name="inv_all")

        nc.scalar.dma_start(out=o_scale[:], in_=overlap_scale.rearrange("a b -> (a b)").partition_broadcast(P))
        nc.scalar.dma_start(out=f_scale[:], in_=field_scale.rearrange("(p m) b -> p m b", m=8))
        nc.scalar.dma_start(out=area_rows[:], in_=area.rearrange("(c p) -> c p", p=P))

        w_bytes = [keep.tile([P, 2, K], U8, name="w_bytes%d" % i) for i in range(6)]
        f_bytes = [keep.tile([P, 2, K], U8, name="f_bytes%d" % i) for i in range(4)]
        f_rows = field_bytes.rearrange("(p m) k -> p m k", m=8)

        def load_w(i, lo, hi):
            src = overlap_bytes[256 * i : 256 * i + 256, lo:hi].rearrange("(t p) k -> p t k", p=P)
            nc.sync.dma_start(out=w_bytes[i][:, :, lo:hi], in_=src)

        def load_f(i):
            nc.sync.dma_start(out=f_bytes[i][:], in_=f_rows[:, 2 * i : 2 * i + 2, :])

        load_w(0, 0, 512)
        load_w(0, 512, K)
        for u in UNITS[1:]:
            if u == "W2":
                nc.sync.dma_start(out=clim_all[:], in_=clim.partition_broadcast(P))
            if u[0] == "W":
                load_w(int(u[1:]), 0, K)
            elif u[1:] in "0246":
                load_f(int(u[1:]) // 2)

        w_codes = [keep.tile([P, 4, 256], U32, align_bytes=64, name="w_codes%d" % i) for i in range(6)]
        w_planes = [keep.tile([P, 4, 256], U8, align_bytes=64, name="w_planes%d" % i) for i in range(6)]
        f_codes = [keep.tile([P, 4, P], U32, align_bytes=64, name="f_codes%d" % m) for m in range(8)]
        f_planes = [keep.tile([P, 4, P], U8, align_bytes=64, name="f_planes%d" % m) for m in range(8)]

        chunks = []
        for u in UNITS:
            chunks += [(u[0], int(u[1:]), c) for c in range(4 if u[0] == "W" else 2)]
        n_chunks = len(chunks)
        wide, bank, grouped = {}, {}, {}

        def on_vector(c, h):
            share = CFG['v'][0] if c < CFG['b'][0] else CFG['v'][1] if c < CFG['b'][1] else CFG['v'][2]
            j = 2 * c + 1 - h
            return (j + 1) * share // 8 > j * share // 8

        def widen(c, h):
            kind, i, part = chunks[c]
            t = wide_pool.tile([P, 512], BF16, align_bytes=64, name="wide")
            for q in range(4):
                if kind == "W":
                    b = 4 * part + q
                    src = w_bytes[i][:, h, P * b : P * b + P]
                    col = o_scale[:, 16 * (2 * i + h) + b : 16 * (2 * i + h) + b + 1]
                else:
                    b = 4 * (2 * part + h) + q
                    src = f_bytes[i // 2][:, i % 2, P * b : P * b + P]
                    col = f_scale[:, i, b : b + 1]
                dst = t[:, P * q : P * q + P]
                if on_vector(c, h):
                    nc.vector.tensor_scalar(
                        out=t[:].rearrange("p (e w i) -> p w e i", e=2, i=2)[:, 32 * q : 32 * q + 32] if CFG["contig"] else dst,
                        in0=src.bitcast(FP8).rearrange("p (w e i) -> p w e i", e=2, i=2) if CFG["contig"] else src.bitcast(FP8),
                        scalar1=col, scalar2=None, op0=MULT,
                    )
                else:
                    nc.scalar.activation(out=dst, in_=src.bitcast(FP8), func=COPY, scale=col)
            wide[c, h] = t

        def turn(c):
            t = psum_tr.tile([P, 2, 2, P], F32, name="bank")
            for h in (0, 1):
                words = wide[c, h][:].bitcast(F32)
                split = CFG['contig'] and on_vector(c, h)
                for e in (0, 1):
                    nc.tensor.transpose(t[:, h, e, :], words[:, P * e : P * e + P] if split else words[:, e::2], ident[:])
            bank[c] = t

        def leave(c):
            if c % 2 == 0:
                grouped[c] = group_pool.tile([P, 2, 1024], BF16, align_bytes=64, name="group")
            t = grouped[c - c % 2]
            dst = t[:, c % 2, :].bitcast(F32).rearrange("p (h r e) -> p h r e", h=2, e=2)
            if c in CFG['x']:
                nc.vector.tensor_copy(out=dst, in_=bank[c][:].rearrange("p h e r -> p h r e"))
            else:
                nc.scalar.copy(out=dst, in_=bank[c][:].rearrange("p h e r -> p h r e"))

        def multiply(ms, qs):
            acc = psum_acc.tile([P, 2, 256], F32, name="acc")
            for half, (m, q) in enumerate([(m, q) for m in ms for q in qs]):
                for g in range(4):
                    nc.tensor.matmul_mx(
                        out=acc[:, half, :],
                        lhsT=f_codes[m][:, g, :].bitcast(FP8X4),
                        lhsT_scale=f_planes[m][:, g, :],
                        rhs=w_codes[q][:, g, :].bitcast(FP8X4),
                        rhs_scale=w_planes[q][:, g, :],
                        start=(g == 0),
                        stop=(g == 3),
                    )
            return acc

        ready, done_f, done_w = [], [], []

        def quantize(c):
            kind, i, part = chunks[c]
            if kind == "W":
                codes = w_codes[i][:, part : part + 2, :].rearrange("p g r -> p (g r)")
                planes = w_planes[i][:, part : part + 2, :].rearrange("p g r -> p (g r)")
            else:
                codes = f_codes[i][:].rearrange("p g r -> p (g r)")
                planes = f_planes[i][:].rearrange("p g r -> p (g r)")
            nc.vector.quantize_mx(
                out=codes.bitcast(FP8X4), scales=planes, in_=grouped[c][:].rearrange("p c x -> p (c x)")
            )
            if kind == "W" and part == 2:
                done_w.append(i)
                ready.extend([((m, m + 1), (i,)) for m in done_f if m % 2 == 0])
            if kind == "F":
                done_f.append(i)
                if i >= 6:
                    ready.extend([((i,), (2 * j, 2 * j + 1)) for j in range(3)])
                elif i % 2 == 1:
                    ready.extend([((i - 1, i), (q,)) for q in done_w])

        def over_columns(row, qs, n_ms):
            cols = row[:, 256 * qs[0] : 256 * qs[0] + 256 * len(qs)]
            if n_ms == 2:
                return cols.unsqueeze(1).to_broadcast([P, 2, 256])
            return cols.rearrange("p (q n) -> p q n", q=2)

        results, order = {}, {}

        def scale(task, acc):
            ms, qs = task
            res = res_pool.tile([P, 2, 256], F32, name="res")
            nc.vector.tensor_tensor(out=res[:], in0=acc[:], in1=over_columns(inv_all, qs, len(ms)), op=MULT)
            results[task] = res
            order[task] = len(order)

        out_rows = out.rearrange("(p m) n -> p m n", m=8)

        def shift(task):
            ms, qs = task
            res = results[task]
            adder = nc.gpsimd if order[task] in CFG['g'] else nc.vector
            adder.tensor_tensor(out=res[:], in0=res[:], in1=over_columns(clim_all, qs, len(ms)), op=ADD)
            cols = slice(256 * qs[0], 256 * qs[0] + 256 * len(qs))
            if len(ms) == 2:
                nc.sync.dma_start(out=out_rows[:, ms[0] : ms[0] + 2, cols], in_=res[:])
            else:
                nc.sync.dma_start(out=out_rows[:, ms[0], cols], in_=res[:].rearrange("p q n -> p (q n)"))

        def invert_area():
            nc.vector.tensor_copy(out=area_f32[0:12, :], in_=area_rows[:])
            t = psum_tr.tile([P, 4, P], F32, name="bank")
            nc.tensor.transpose(t[:, 0, :], area_f32[:], ident[:])
            nc.vector.reciprocal(out=inv_cols[:], in_=t[:, 0, 0:12])

        def spread_inverse():
            for j in range(3):
                t = psum_tr.tile([P, 4, P], F32, name="bank")
                for c in range(4):
                    col = 4 * j + c
                    nc.tensor.transpose(t[:, c, :], inv_cols[:, col : col + 1].to_broadcast([P, P]), ident[:])
                nc.scalar.copy(out=inv_all[:, 512 * j : 512 * j + 512], in_=t[:].rearrange("p c r -> p (c r)"))

        with tc.manual_schedule():
            TL, EL, QL, R = CFG["TL"], CFG["EL"], CFG["QL"], CFG["R"]
            fresh, last_shift, older = [], [], []
            credit = 0.0
            step = 0
            while step < n_chunks + QL + 1 or ready or fresh or last_shift or older:
                if step == CFG["inv"]:
                    invert_area()
                if step == CFG["inv"] + 3:
                    spread_inverse()
                groups = [(step, h) for h in (0, 1)] if step < n_chunks else []
                sg = [g for g in groups if not on_vector(g[0], g[1])]
                vg = [g for g in groups if on_vector(g[0], g[1])]
                if CFG["sfirst"]:
                    for g in sg[:1]:
                        widen(g[0], g[1])
                    sg = sg[1:]
                if 0 <= step - EL < n_chunks:
                    leave(step - EL)
                for g in sg:
                    widen(g[0], g[1])
                able = len(ready)
                c = step - QL
                outs = [(shift, (t,)) for t in last_shift] + [(scale, z) for z in fresh]
                last_shift = [z[0] for z in fresh]
                quant = [(quantize, (c - 1,))] if 0 <= c < n_chunks and c % 2 == 1 else []
                wid = [(widen, g) for g in vg]
                for part in CFG["vorder"]:
                    for fn, args in {"w": wid, "q": quant, "o": outs}[part]:
                        fn(*args)
                fresh = []
                c = step - TL
                turns = list(range(c - R + 1, c + 1)) if 0 <= c < n_chunks and c % R == R - 1 else []
                if CFG["tfirst"]:
                    for k in turns:
                        turn(k)
                credit = min(credit + (CFG["pace"][0] if step < CFG["ps"] else CFG["pace"][1]), 3.0) if ready else 0.5
                while able > 0 and credit >= 1.0:
                    task = ready.pop(0)
                    able -= 1
                    credit -= 1.0
                    fresh.append((task, multiply(*task)))
                if not CFG["tfirst"]:
                    for k in turns:
                        turn(k)
                step += 1
